import numpy as np
import ml_dtypes


def mxq(x, axis, fmt="e4m3"):
    dtype, down = {"e4m3": (ml_dtypes.float8_e4m3fn, 7), "e5m2": (ml_dtypes.float8_e5m2, 14)}[fmt]
    v = np.moveaxis(np.asarray(x, np.float32).astype(ml_dtypes.bfloat16).astype(np.float64), axis, -1)
    blocks = v.reshape(v.shape[:-1] + (-1, 32))
    amax = np.abs(blocks).max(-1, keepdims=True)
    byte = np.maximum(np.where(amax > 0, np.frexp(amax)[1] - 1 + 127, 0) - down, 1)
    scale = np.exp2(byte - 127.0)
    codes = (blocks / scale).astype(np.float32).astype(dtype).astype(np.float64)
    return np.moveaxis((codes * scale).reshape(v.shape), -1, axis)


WIDE = False


def mx_kscale(k):
    if not WIDE:
        return np.ones(k)
    levels = np.array([10, -10, 5, -5, 0])
    if k % 512:
        return np.exp2(np.random.permutation(np.resize(levels, k // 32))).repeat(32)
    a = np.empty((k // 512, 16))
    for p in range(k // 512):
        a[p, :8] = np.random.permutation(np.resize(levels, 8))
        for g in range(8):
            far = levels[np.abs(levels - a[p, g]) >= 10]
            a[p, g + 8] = far[np.random.randint(len(far))]
    return np.exp2(a.ravel()).repeat(32)


def f64(x):
    return np.asarray(x).astype(np.float64)


def striped(idx):
    return np.tile(idx.reshape(-1, 16).T, (8, 1)).astype(np.uint16)


def unstriped(offs):
    return offs[:16].T.reshape(-1).astype(np.int64)


def pack_weight(w):
    k, n = w.shape
    w = f64(np.asarray(w, np.float32).astype(ml_dtypes.bfloat16)).reshape(k // 32, 32, n)
    amax = np.abs(w).max(1)
    byte = np.clip(np.where(amax > 0, np.frexp(amax)[1] - 1 + 127 - 7, 1), 1, 254)
    scaled = (w * np.exp2(127.0 - byte)[:, None, :]).reshape(k, n).astype(np.float32)
    words = np.ascontiguousarray(scaled.reshape(k // 512, 128, 4, n).transpose(0, 1, 3, 2)).astype(ml_dtypes.float8_e4m3fn).view(np.uint8)
    return words, np.ascontiguousarray(byte.astype(np.uint8).reshape(k // 512, 16, n))


def unpack_weight(words, scales):
    g, p, n, _ = words.shape
    vals = np.ascontiguousarray(words).view(ml_dtypes.float8_e4m3fn).astype(np.float64) * np.repeat(np.exp2(scales.astype(np.float64) - 127.0), 8, axis=1)[..., None]
    return vals.transpose(0, 1, 3, 2).reshape(g * 512, n)


def planes(y):
    n, m = y.shape
    v = y.astype(np.float32).astype(ml_dtypes.bfloat16).astype(np.float64).reshape(n // 32, 32, m)
    top = np.abs(v).max(1)
    byte = np.clip(np.where(top > 0, np.frexp(top)[1] - 1 + 127 - 7, 1), 1, 254)
    codes = (v * np.exp2(127.0 - byte)[:, None, :]).reshape(n, m).astype(np.float32).astype(ml_dtypes.float8_e4m3fn).view(np.uint8)
    words = codes.reshape(n // 512, 128, 4, m).transpose(0, 1, 3, 2)
    return np.ascontiguousarray(words), np.ascontiguousarray(byte.astype(np.uint8).reshape(n // 512, 16, m))


K, T, S, H, N = 512, 1024, 512, 512, 512


def setup_inputs():
    n = np.random.standard_normal
    s = mx_kscale(K)[:, None]
    u = mx_kscale(H)
    packed_xT = pack_weight(n((K, T)) * s)
    packed_w3 = pack_weight(n((H, N)) / np.sqrt(H) / u[:, None])
    packed_w4 = pack_weight(n((K, N)) / np.sqrt(K) / s)
    return {
        "x_words": packed_xT[0],
        "x_scales": packed_xT[1],
        "w1": (n((K, H)) / np.sqrt(2 * K) / s * u).astype(np.float32),
        "w2": (n((K, H)) / np.sqrt(2 * K) / s * u).astype(np.float32),
        "w3_words": packed_w3[0],
        "w3_scales": packed_w3[1],
        "w4_words": packed_w4[0],
        "w4_scales": packed_w4[1],
        "offs": striped(np.random.permutation(T)[:S]),
        "dst": striped(np.random.permutation(T)[:S]),
    }


def reference(x_words, x_scales, w1, w2, w3_words, w3_scales, w4_words, w4_scales, offs, dst):
    xq = unpack_weight(x_words, x_scales)[:, unstriped(offs)]
    x_dst = unpack_weight(x_words, x_scales)[:, unstriped(dst)]
    y = mxq(f64(w1), 0, "e4m3").T @ xq + mxq(f64(w2), 0, "e4m3").T @ x_dst
    h = np.maximum(y, 0.2 * y)
    e = np.tanh(unpack_weight(w3_words, w3_scales).T @ mxq(h, 0, "e4m3"))
    v = unpack_weight(w4_words, w4_scales).T @ xq
    out_0 = e * v
    return (out_0,) + planes(out_0)

@@ -1,0 +1,200 @@
+from contextlib import ExitStack
+
+import concourse.mybir as mybir
+
+FLOPS = 4 * 2 * 512 * 512 * 512
+
+F32 = mybir.dt.float32
+BF16 = mybir.dt.bfloat16
+I32 = mybir.dt.int32
+U32 = mybir.dt.uint32
+U16 = mybir.dt.uint16
+U8 = mybir.dt.uint8
+FP8X4 = mybir.dt.float8_e4m3fn_x4
+ACT = mybir.ActivationFunctionType
+ALU = mybir.AluOpType
+
+P = 128
+PACK = 4
+NODES = 1024
+EDGES = 512
+WIDTH = 512
+CHUNK = 128
+CHUNKS = EDGES // CHUNK
+HALF = WIDTH // 2
+W4_ROW = 4
+
+
+def tile_picked_zgatt_tanh_po_kernel(
+    tc, x_words, x_scales, w1, w2, w3_words, w3_scales, w4_words, w4_scales, offs, dst, out_0, out_1, out_2
+):
+    nc = tc.nc
+    with ExitStack() as ctx:
+        sb = ctx.enter_context(tc.tile_pool(name="sb", bufs=1))
+        ps = ctx.enter_context(tc.psum_pool(name="ps", bufs=1))
+
+        def tile(name, shape, dtype):
+            return sb.tile(shape, dtype, name=name, align_bytes=64)
+
+        def as_words(packed):
+            return packed[0].rearrange("p n t -> p (n t)").bitcast(I32)
+
+        def load_scale_rows(engine, plane, row, scales):
+            for q in range(4):
+                engine.dma_start(
+                    out=plane[32 * q + row : 32 * q + row + 4, :].bitcast(I32),
+                    in_=scales[0, 4 * q : 4 * q + 4, :].bitcast(I32),
+                )
+
+        src_list = sb.tile([P, EDGES // 16], U16, name="src_list")
+        dst_list = sb.tile([P, EDGES // 16], U16, name="dst_list")
+        x_plane = tile("x_plane", [P, NODES], U8)
+        x_table = tile("x_table", [P, NODES], U32)
+        w34_plane = tile("w34_plane", [P, WIDTH], U8)
+        nc.vector.memset(x_plane[:].bitcast(I32), 0)
+        nc.gpsimd.memset(w34_plane[:].bitcast(I32), 0)
+        nc.sync.dma_start(src_list[:], offs)
+        nc.sync.dma_start(dst_list[:], dst)
+        load_scale_rows(nc.scalar, x_plane, 0, x_scales)
+
+        raw = {}
+
+        def load_half(which, w, half):
+            t = tile("raw%d%d" % (which, half), [P, PACK, HALF], F32)
+            nc.sync.dma_start(out=t[:], in_=w.rearrange("(p j) c -> p j c", j=PACK)[:, :, half * HALF : (half + 1) * HALF])
+            raw[which, half] = t
+
+        load_half(1, w1, 0)
+        nc.sync.dma_start(out=x_table[:].bitcast(I32), in_=as_words(x_words))
+        load_half(1, w1, 1)
+        load_half(2, w2, 0)
+        load_scale_rows(nc.sync, w34_plane, 0, w3_scales)
+        load_half(2, w2, 1)
+        load_scale_rows(nc.sync, w34_plane, W4_ROW, w4_scales)
+        w3_raw = tile("w3_raw", [P, WIDTH], U32)
+        w4_raw = tile("w4_raw", [P, WIDTH], U32)
+        nc.sync.dma_start(out=w3_raw[:].bitcast(I32), in_=as_words(w3_words))
+        nc.sync.dma_start(out=w4_raw[:].bitcast(I32), in_=as_words(w4_words))
+
+        xs_scale = tile("xs_scale", [P, EDGES], U8)
+        xd_scale = tile("xd_scale", [P, EDGES], U8)
+        xs_codes = tile("xs_codes", [P, EDGES], U32)
+        xd_codes = tile("xd_codes", [P, EDGES], U32)
+        nc.vector.tensor_copy(xs_scale[:], x_plane[:].indirect(src_list[:]))
+        nc.vector.tensor_copy(xd_scale[:], x_plane[:].indirect(dst_list[:]))
+        nc.vector.tensor_copy(xs_codes[:], x_table[:].indirect(src_list[:]))
+        nc.vector.tensor_copy(xd_codes[:], x_table[:].indirect(dst_list[:]))
+
+        grouped = {w: tile("grouped%d" % w, [P, PACK, P, PACK], BF16) for w in (1, 2)}
+        w_codes = {w: tile("w_codes%d" % w, [P, WIDTH], U32) for w in (1, 2)}
+        w_scale = {w: tile("w_scale%d" % w, [P, WIDTH], U8) for w in (1, 2)}
+
+        def round_part(copy, which, half, m0, m1):
+            base = half * (HALF // PACK)
+            copy(
+                out=grouped[which][:, :, base + m0 : base + m1, :].rearrange("p t m j -> p m j t"),
+                in_=raw[which, half][:, :, PACK * m0 : PACK * m1].rearrange("p j (m t) -> p m j t", t=PACK),
+            )
+
+        round_part(nc.scalar.copy, 1, 0, 0, 64)
+        round_part(nc.scalar.copy, 1, 1, 0, 64)
+        nc.vector.quantize_mx(
+            out=w_codes[1][:].bitcast(FP8X4), scales=w_scale[1][:], in_=grouped[1][:].rearrange("p t m j -> p (t m j)")
+        )
+        round_part(nc.scalar.copy, 2, 0, 0, 64)
+        round_part(nc.scalar.copy, 2, 1, 0, 24)
+        round_part(nc.vector.tensor_copy, 2, 1, 24, 64)
+
+        acc = [ps.tile([P, PACK, CHUNK], F32, name="y%d" % c, tag="acc%d" % c) for c in range(CHUNKS)]
+
+        def cols(i):
+            return slice(i * P, (i + 1) * P)
+
+        def passes(bank, codes, scale, row, x_codes, x_scale, opens, closes):
+            for t in range(PACK):
+                nc.tensor.matmul_mx(
+                    out=bank[:, t, :],
+                    lhsT=codes[:, cols(t)].bitcast(FP8X4),
+                    lhsT_scale=scale[row:P, cols(t)],
+                    rhs=x_codes.bitcast(FP8X4),
+                    rhs_scale=x_scale,
+                    start=opens(t),
+                    stop=closes(t),
+                )
+
+        for c in range(CHUNKS):
+            passes(acc[c], w_codes[1], w_scale[1], 0, xs_codes[:, cols(c)], xs_scale[:, cols(c)], lambda t: t == 0, lambda t: False)
+        for t in range(PACK):
+            nc.vector.quantize_mx(
+                out=w_codes[2][:, cols(t)].bitcast(FP8X4),
+                scales=w_scale[2][:, cols(t)],
+                in_=grouped[2][:, t, :, :].rearrange("p m j -> p (m j)"),
+            )
+        for c in range(CHUNKS):
+            passes(acc[c], w_codes[2], w_scale[2], 0, xd_codes[:, cols(c)], xd_scale[:, cols(c)], lambda t: False, lambda t: t == PACK - 1)
+
+        w3_codes = tile("w3_codes", [P, WIDTH], U32)
+        w4_codes = tile("w4_codes", [P, WIDTH], U32)
+        w34_scale = tile("w34_scale", [P, WIDTH], U8)
+        for dealt, packed in ((w3_codes, w3_raw), (w4_codes, w4_raw)):
+            nc.scalar.copy(
+                out=dealt[:].rearrange("p (t m) -> p m t", t=PACK), in_=packed[:].rearrange("p (m t) -> p m t", t=PACK)
+            )
+        nc.vector.tensor_copy(
+            out=w34_scale[:].rearrange("p (t m) -> p t m", t=PACK), in_=w34_plane[:].rearrange("p (m t) -> p t m", t=PACK)
+        )
+
+        msg = [ps.tile([P, PACK, CHUNK], F32, name="v%d" % c, tag="msg%d" % c) for c in range(CHUNKS)]
+        for c in range(CHUNKS):
+            passes(msg[c], w4_codes, w34_scale, W4_ROW, xs_codes[:, cols(c)], xs_scale[:, cols(c)], lambda t: True, lambda t: True)
+
+        out_codes = tile("out_codes", [P, EDGES], U32)
+        out_scale = tile("out_scale", [P, EDGES], U8)
+        hidden, score, result, rounded = {}, {}, {}, {}
+        out_rows = out_0.rearrange("(p t) j -> p t j", t=PACK)
+        out_words = as_words(out_1)
+
+        def leaky(c):
+            y = acc[c][:].rearrange("p t n -> p n t")
+            fifth = tile("fifth%d" % c, [P, CHUNK, PACK], F32)
+            nc.scalar.activation(out=fifth[:], in_=y, func=ACT.Copy, scale=0.2)
+            hidden[c] = tile("hidden%d" % c, [P, CHUNK, PACK], BF16)
+            nc.vector.tensor_tensor(out=hidden[c][:], in0=y, in1=fifth[:], op=ALU.max)
+
+        def scores(c):
+            h_codes = tile("h_codes%d" % c, [P, CHUNK], U32)
+            h_scale = tile("h_scale%d" % c, [P, CHUNK], U8)
+            nc.vector.quantize_mx(out=h_codes[:].bitcast(FP8X4), scales=h_scale[:], in_=hidden[c][:].rearrange("p n t -> p (n t)"))
+            bank = ps.tile([P, PACK, CHUNK], F32, name="e%d" % c, tag="acc%d" % c)
+            passes(bank, w3_codes, w34_scale, 0, h_codes[:], h_scale[:], lambda t: True, lambda t: True)
+            score[c] = tile("score%d" % c, [P, PACK, CHUNK], F32)
+            nc.scalar.activation(out=score[c][:], in_=bank[:], func=ACT.Tanh)
+
+        def weigh(c):
+            result[c] = tile("result%d" % c, [P, PACK, CHUNK], F32)
+            nc.vector.tensor_tensor(out=result[c][:], in0=msg[c][:], in1=score[c][:], op=ALU.mult)
+            nc.sync.dma_start(out=out_rows[:, :, cols(c)], in_=result[c][:])
+            rounded[c] = tile("rounded%d" % c, [P, CHUNK, PACK], BF16)
+            copy = nc.scalar.copy if c < 2 else nc.vector.tensor_copy
+            copy(
+                out=rounded[c][:].rearrange("p (g i) t -> p g t i", i=4),
+                in_=result[c][:].rearrange("p t (g i) -> p g t i", i=4),
+            )
+
+        def hand_on(c):
+            nc.vector.quantize_mx(
+                out=out_codes[:, cols(c)].bitcast(FP8X4), scales=out_scale[:, cols(c)], in_=rounded[c][:].rearrange("p n t -> p (n t)")
+            )
+            nc.sync.dma_start(out=out_words[:, cols(c)], in_=out_codes[:, cols(c)].bitcast(I32))
+
+        stages = (leaky, scores, weigh, hand_on)
+        for step in range(CHUNKS + len(stages) - 1):
+            for lag, stage in enumerate(stages):
+                if 0 <= step - lag < CHUNKS:
+                    stage(step - lag)
+
+        for q in range(4):
+            engine = nc.sync if q % 2 == 0 else nc.scalar
+            engine.dma_start(
+                out=out_2[0, 4 * q : 4 * q + 4, :].bitcast(I32), in_=out_scale[32 * q : 32 * q + 4, :].bitcast(I32)
+            )

@@ -31,6 +31,7 @@ def tile_picked_zgatt_tanh_po_kernel(
     nc = tc.nc
     with ExitStack() as ctx:
         sb = ctx.enter_context(tc.tile_pool(name="sb", bufs=1))
+        reuse = ctx.enter_context(tc.tile_pool(name="reuse", bufs=1))
         ps = ctx.enter_context(tc.psum_pool(name="ps", bufs=1))
 
         def tile(name, shape, dtype):
@@ -51,11 +52,10 @@ def tile_picked_zgatt_tanh_po_kernel(
         x_plane = tile("x_plane", [P, NODES], U8)
         x_table = tile("x_table", [P, NODES], U32)
         w34_plane = tile("w34_plane", [P, WIDTH], U8)
-        nc.vector.memset(x_plane[:].bitcast(I32), 0)
+        nc.gpsimd.memset(x_plane[:].bitcast(I32), 0)
         nc.gpsimd.memset(w34_plane[:].bitcast(I32), 0)
         nc.sync.dma_start(src_list[:], offs)
         nc.sync.dma_start(dst_list[:], dst)
-        load_scale_rows(nc.scalar, x_plane, 0, x_scales)
 
         raw = {}
 
@@ -65,12 +65,13 @@ def tile_picked_zgatt_tanh_po_kernel(
             raw[which, half] = t
 
         load_half(1, w1, 0)
+        load_scale_rows(nc.sync, x_plane, 0, x_scales)
         nc.sync.dma_start(out=x_table[:].bitcast(I32), in_=as_words(x_words))
         load_half(1, w1, 1)
         load_half(2, w2, 0)
         load_scale_rows(nc.sync, w34_plane, 0, w3_scales)
         load_half(2, w2, 1)
-        load_scale_rows(nc.sync, w34_plane, W4_ROW, w4_scales)
+        load_scale_rows(nc.gpsimd, w34_plane, W4_ROW, w4_scales)
         w3_raw = tile("w3_raw", [P, WIDTH], U32)
         w4_raw = tile("w4_raw", [P, WIDTH], U32)
         nc.sync.dma_start(out=w3_raw[:].bitcast(I32), in_=as_words(w3_words))
@@ -78,14 +79,17 @@ def tile_picked_zgatt_tanh_po_kernel(
 
         xs_scale = tile("xs_scale", [P, EDGES], U8)
         xd_scale = tile("xd_scale", [P, EDGES], U8)
-        xs_codes = tile("xs_codes", [P, EDGES], U32)
-        xd_codes = tile("xd_codes", [P, EDGES], U32)
+        xs_codes = [tile("xs_codes0", [P, HALF], U32)]
+        xd_codes = [tile("xd_codes0", [P, HALF], U32)]
         nc.vector.tensor_copy(xs_scale[:], x_plane[:].indirect(src_list[:]))
         nc.vector.tensor_copy(xd_scale[:], x_plane[:].indirect(dst_list[:]))
-        nc.vector.tensor_copy(xs_codes[:], x_table[:].indirect(src_list[:]))
-        nc.vector.tensor_copy(xd_codes[:], x_table[:].indirect(dst_list[:]))
+        nc.vector.tensor_copy(xs_codes[0][:], x_table[:].indirect(src_list[:, 0:16]))
+        nc.vector.tensor_copy(xd_codes[0][:], x_table[:].indirect(dst_list[:, 0:16]))
 
-        grouped = {w: tile("grouped%d" % w, [P, PACK, P, PACK], BF16) for w in (1, 2)}
+        grouped = {
+            1: tile("grouped1", [P, PACK, P, PACK], BF16),
+            2: reuse.tile([P, PACK, P, PACK], BF16, name="grouped2", align_bytes=64, offset=0),
+        }
         w_codes = {w: tile("w_codes%d" % w, [P, WIDTH], U32) for w in (1, 2)}
         w_scale = {w: tile("w_scale%d" % w, [P, WIDTH], U8) for w in (1, 2)}
 
@@ -122,20 +126,23 @@ def tile_picked_zgatt_tanh_po_kernel(
                     stop=closes(t),
                 )
 
-        for c in range(CHUNKS):
-            passes(acc[c], w_codes[1], w_scale[1], 0, xs_codes[:, cols(c)], xs_scale[:, cols(c)], lambda t: t == 0, lambda t: False)
         for t in range(PACK):
             nc.vector.quantize_mx(
                 out=w_codes[2][:, cols(t)].bitcast(FP8X4),
                 scales=w_scale[2][:, cols(t)],
                 in_=grouped[2][:, t, :, :].rearrange("p m j -> p (m j)"),
             )
+        xs_codes.append(reuse.tile([P, HALF], U32, name="xs_codes1", align_bytes=64, offset=0))
+        xd_codes.append(reuse.tile([P, HALF], U32, name="xd_codes1", align_bytes=64, offset=1024))
+        nc.vector.tensor_copy(xs_codes[1][:], x_table[:].indirect(src_list[:, 16:32]))
+        nc.vector.tensor_copy(xd_codes[1][:], x_table[:].indirect(dst_list[:, 16:32]))
         for c in range(CHUNKS):
-            passes(acc[c], w_codes[2], w_scale[2], 0, xd_codes[:, cols(c)], xd_scale[:, cols(c)], lambda t: False, lambda t: t == PACK - 1)
+            passes(acc[c], w_codes[1], w_scale[1], 0, xs_codes[c // 2][:, cols(c % 2)], xs_scale[:, cols(c)], lambda t: t == 0, lambda t: False)
+            passes(acc[c], w_codes[2], w_scale[2], 0, xd_codes[c // 2][:, cols(c % 2)], xd_scale[:, cols(c)], lambda t: False, lambda t: t == PACK - 1)
 
         w3_codes = tile("w3_codes", [P, WIDTH], U32)
         w4_codes = tile("w4_codes", [P, WIDTH], U32)
-        w34_scale = tile("w34_scale", [P, WIDTH], U8)
+        w34_scale = reuse.tile([P, WIDTH], U8, name="w34_scale", align_bytes=64, offset=2048)
         for dealt, packed in ((w3_codes, w3_raw), (w4_codes, w4_raw)):
             nc.scalar.copy(
                 out=dealt[:].rearrange("p (t m) -> p m t", t=PACK), in_=packed[:].rearrange("p (m t) -> p m t", t=PACK)
@@ -145,8 +152,6 @@ def tile_picked_zgatt_tanh_po_kernel(
         )
 
         msg = [ps.tile([P, PACK, CHUNK], F32, name="v%d" % c, tag="msg%d" % c) for c in range(CHUNKS)]
-        for c in range(CHUNKS):
-            passes(msg[c], w4_codes, w34_scale, W4_ROW, xs_codes[:, cols(c)], xs_scale[:, cols(c)], lambda t: True, lambda t: True)
 
         out_codes = tile("out_codes", [P, EDGES], U32)
         out_scale = tile("out_scale", [P, EDGES], U8)
@@ -167,6 +172,7 @@ def tile_picked_zgatt_tanh_po_kernel(
             nc.vector.quantize_mx(out=h_codes[:].bitcast(FP8X4), scales=h_scale[:], in_=hidden[c][:].rearrange("p n t -> p (n t)"))
             bank = ps.tile([P, PACK, CHUNK], F32, name="e%d" % c, tag="acc%d" % c)
             passes(bank, w3_codes, w34_scale, 0, h_codes[:], h_scale[:], lambda t: True, lambda t: True)
+            passes(msg[c], w4_codes, w34_scale, W4_ROW, xs_codes[c // 2][:, cols(c % 2)], xs_scale[:, cols(c)], lambda t: True, lambda t: True)
             score[c] = tile("score%d" % c, [P, PACK, CHUNK], F32)
             nc.scalar.activation(out=score[c][:], in_=bank[:], func=ACT.Tanh)
 
@@ -175,7 +181,7 @@ def tile_picked_zgatt_tanh_po_kernel(
             nc.vector.tensor_tensor(out=result[c][:], in0=msg[c][:], in1=score[c][:], op=ALU.mult)
             nc.sync.dma_start(out=out_rows[:, :, cols(c)], in_=result[c][:])
             rounded[c] = tile("rounded%d" % c, [P, CHUNK, PACK], BF16)
-            copy = nc.scalar.copy if c < 2 else nc.vector.tensor_copy
+            copy = nc.scalar.copy if c < CHUNKS - 1 else nc.vector.tensor_copy
             copy(
                 out=rounded[c][:].rearrange("p (g i) t -> p g t i", i=4),
                 in_=result[c][:].rearrange("p t (g i) -> p g t i", i=4),

@@ -16,13 +16,21 @@ ALU = mybir.AluOpType
 
 P = 128
 PACK = 4
+QUADRANTS = 4
 NODES = 1024
 EDGES = 512
 WIDTH = 512
 CHUNK = 128
 CHUNKS = EDGES // CHUNK
-HALF = WIDTH // 2
-W4_ROW = 4
+LIST_ROWS = 16
+W3_ROW, W4_ROW = 0, 4
+SLOPE = 0.2
+
+W1_HEAD = 32
+W2_HALF = 64
+W2_SCALAR = 20
+
+ROUNDED_AT = {1: 4096, 2: 0}
 
 
 def tile_picked_zgatt_tanh_po_kernel(
@@ -30,176 +38,193 @@ def tile_picked_zgatt_tanh_po_kernel(
 ):
     nc = tc.nc
     with ExitStack() as ctx:
-        sb = ctx.enter_context(tc.tile_pool(name="sb", bufs=1))
-        reuse = ctx.enter_context(tc.tile_pool(name="reuse", bufs=1))
-        ps = ctx.enter_context(tc.psum_pool(name="ps", bufs=1))
+        held = ctx.enter_context(tc.tile_pool(name="held", bufs=1))
+        shared = ctx.enter_context(tc.tile_pool(name="shared", bufs=1))
+        psum = ctx.enter_context(tc.psum_pool(name="psum", bufs=1))
 
         def tile(name, shape, dtype):
-            return sb.tile(shape, dtype, name=name, align_bytes=64)
+            return held.tile(shape, dtype, name=name, align_bytes=64)
+
+        def tile_at(offset, name, shape, dtype):
+            return shared.tile(shape, dtype, name=name, align_bytes=64, offset=offset)
 
         def as_words(packed):
             return packed[0].rearrange("p n t -> p (n t)").bitcast(I32)
 
-        def load_scale_rows(engine, plane, row, scales):
-            for q in range(4):
-                engine.dma_start(
-                    out=plane[32 * q + row : 32 * q + row + 4, :].bitcast(I32),
-                    in_=scales[0, 4 * q : 4 * q + 4, :].bitcast(I32),
-                )
-
-        src_list = sb.tile([P, EDGES // 16], U16, name="src_list")
-        dst_list = sb.tile([P, EDGES // 16], U16, name="dst_list")
-        x_plane = tile("x_plane", [P, NODES], U8)
-        x_table = tile("x_table", [P, NODES], U32)
-        w34_plane = tile("w34_plane", [P, WIDTH], U8)
-        nc.gpsimd.memset(x_plane[:].bitcast(I32), 0)
-        nc.gpsimd.memset(w34_plane[:].bitcast(I32), 0)
-        nc.sync.dma_start(src_list[:], offs)
-        nc.sync.dma_start(dst_list[:], dst)
-
-        raw = {}
-
-        def load_half(which, w, half):
-            t = tile("raw%d%d" % (which, half), [P, PACK, HALF], F32)
-            nc.sync.dma_start(out=t[:], in_=w.rearrange("(p j) c -> p j c", j=PACK)[:, :, half * HALF : (half + 1) * HALF])
-            raw[which, half] = t
-
-        load_half(1, w1, 0)
-        load_scale_rows(nc.sync, x_plane, 0, x_scales)
-        nc.sync.dma_start(out=x_table[:].bitcast(I32), in_=as_words(x_words))
-        load_half(1, w1, 1)
-        load_half(2, w2, 0)
-        load_scale_rows(nc.sync, w34_plane, 0, w3_scales)
-        load_half(2, w2, 1)
-        load_scale_rows(nc.gpsimd, w34_plane, W4_ROW, w4_scales)
-        w3_raw = tile("w3_raw", [P, WIDTH], U32)
-        w4_raw = tile("w4_raw", [P, WIDTH], U32)
-        nc.sync.dma_start(out=w3_raw[:].bitcast(I32), in_=as_words(w3_words))
-        nc.sync.dma_start(out=w4_raw[:].bitcast(I32), in_=as_words(w4_words))
-
-        xs_scale = tile("xs_scale", [P, EDGES], U8)
-        xd_scale = tile("xd_scale", [P, EDGES], U8)
-        xs_codes = [tile("xs_codes0", [P, HALF], U32)]
-        xd_codes = [tile("xd_codes0", [P, HALF], U32)]
-        nc.vector.tensor_copy(xs_scale[:], x_plane[:].indirect(src_list[:]))
-        nc.vector.tensor_copy(xd_scale[:], x_plane[:].indirect(dst_list[:]))
-        nc.vector.tensor_copy(xs_codes[0][:], x_table[:].indirect(src_list[:, 0:16]))
-        nc.vector.tensor_copy(xd_codes[0][:], x_table[:].indirect(dst_list[:, 0:16]))
-
-        grouped = {
-            1: tile("grouped1", [P, PACK, P, PACK], BF16),
-            2: reuse.tile([P, PACK, P, PACK], BF16, name="grouped2", align_bytes=64, offset=0),
-        }
-        w_codes = {w: tile("w_codes%d" % w, [P, WIDTH], U32) for w in (1, 2)}
-        w_scale = {w: tile("w_scale%d" % w, [P, WIDTH], U8) for w in (1, 2)}
-
-        def round_part(copy, which, half, m0, m1):
-            base = half * (HALF // PACK)
-            copy(
-                out=grouped[which][:, :, base + m0 : base + m1, :].rearrange("p t m j -> p m j t"),
-                in_=raw[which, half][:, :, PACK * m0 : PACK * m1].rearrange("p j (m t) -> p m j t", t=PACK),
-            )
-
-        round_part(nc.scalar.copy, 1, 0, 0, 64)
-        round_part(nc.scalar.copy, 1, 1, 0, 64)
-        nc.vector.quantize_mx(
-            out=w_codes[1][:].bitcast(FP8X4), scales=w_scale[1][:], in_=grouped[1][:].rearrange("p t m j -> p (t m j)")
-        )
-        round_part(nc.scalar.copy, 2, 0, 0, 64)
-        round_part(nc.scalar.copy, 2, 1, 0, 24)
-        round_part(nc.vector.tensor_copy, 2, 1, 24, 64)
-
-        acc = [ps.tile([P, PACK, CHUNK], F32, name="y%d" % c, tag="acc%d" % c) for c in range(CHUNKS)]
-
         def cols(i):
             return slice(i * P, (i + 1) * P)
 
-        def passes(bank, codes, scale, row, x_codes, x_scale, opens, closes):
+        def load_scale_rows(engine, scale_tile, row, scales):
+            for q in range(QUADRANTS):
+                engine.dma_start(
+                    out=scale_tile[32 * q + row : 32 * q + row + 4, :].bitcast(I32),
+                    in_=scales[0, 4 * q : 4 * q + 4, :].bitcast(I32),
+                )
+
+        src_list = held.tile([P, EDGES // LIST_ROWS], U16, name="src_list")
+        dst_list = held.tile([P, EDGES // LIST_ROWS], U16, name="dst_list")
+        x_scale_table = tile("x_scale_table", [P, NODES], U8)
+        x_word_table = tile("x_word_table", [P, NODES], U32)
+        w34_scale_raw = tile("w34_scale_raw", [P, WIDTH], U8)
+        nc.gpsimd.memset(x_scale_table[:].bitcast(I32), 0)
+        nc.gpsimd.memset(w34_scale_raw[:].bitcast(I32), 0)
+        nc.sync.dma_start(src_list[:], offs)
+        nc.sync.dma_start(dst_list[:], dst)
+
+        def load_groups(name, w, m0, m1):
+            piece = tile(name, [P, PACK, PACK * (m1 - m0)], F32)
+            nc.sync.dma_start(out=piece[:], in_=w.rearrange("(p j) c -> p j c", j=PACK)[:, :, PACK * m0 : PACK * m1])
+            return piece
+
+        w1_head = load_groups("w1_head", w1, 0, W1_HEAD)
+        load_scale_rows(nc.sync, x_scale_table, 0, x_scales)
+        w1_rest = load_groups("w1_rest", w1, W1_HEAD, P)
+        nc.sync.dma_start(out=x_word_table[:].bitcast(I32), in_=as_words(x_words))
+        w2_low = load_groups("w2_low", w2, 0, W2_HALF)
+        w2_high = load_groups("w2_high", w2, W2_HALF, P)
+        load_scale_rows(nc.gpsimd, w34_scale_raw, W4_ROW, w4_scales)
+        w3_raw = tile("w3_raw", [P, WIDTH], U32)
+        w4_raw = tile("w4_raw", [P, WIDTH], U32)
+        nc.sync.dma_start(out=w3_raw[:].bitcast(I32), in_=as_words(w3_words))
+        load_scale_rows(nc.sync, w34_scale_raw, W3_ROW, w3_scales)
+        nc.sync.dma_start(out=w4_raw[:].bitcast(I32), in_=as_words(w4_words))
+
+        def look_up(gathered, table, entries, first_chunk, chunks):
+            per_chunk = CHUNK // LIST_ROWS
+            offsets = entries[:, first_chunk * per_chunk : (first_chunk + chunks) * per_chunk]
+            nc.vector.tensor_copy(gathered[:], table[:].indirect(offsets))
+
+        src_scale = tile("src_scale", [P, EDGES], U8)
+        dst_scale = tile("dst_scale", [P, EDGES], U8)
+        src_01 = tile("src_01", [P, 2 * CHUNK], U32)
+        look_up(src_scale, x_scale_table, src_list, 0, CHUNKS)
+        look_up(dst_scale, x_scale_table, dst_list, 0, CHUNKS)
+        look_up(src_01, x_word_table, src_list, 0, 2)
+
+        rounded = {w: tile_at(ROUNDED_AT[w], "rounded%d" % w, [P, PACK, P, PACK], BF16) for w in (1, 2)}
+        w_codes = {w: tile("w_codes%d" % w, [P, WIDTH], U32) for w in (1, 2)}
+        w_scale = {w: tile("w_scale%d" % w, [P, WIDTH], U8) for w in (1, 2)}
+
+        def round_groups(copy, w, piece, first, m0, m1):
+            copy(
+                out=rounded[w][:, :, first + m0 : first + m1, :].rearrange("p t m j -> p m j t"),
+                in_=piece[:, :, PACK * m0 : PACK * m1].rearrange("p j (m t) -> p m j t", t=PACK),
+            )
+
+        round_groups(nc.scalar.copy, 1, w1_head, 0, 0, W1_HEAD)
+        round_groups(nc.scalar.copy, 1, w1_rest, W1_HEAD, 0, P - W1_HEAD)
+        nc.vector.quantize_mx(
+            out=w_codes[1][:].bitcast(FP8X4), scales=w_scale[1][:], in_=rounded[1][:].rearrange("p t m j -> p (t m j)")
+        )
+        dst_01 = tile_at(ROUNDED_AT[1], "dst_01", [P, 2 * CHUNK], U32)
+        look_up(dst_01, x_word_table, dst_list, 0, 2)
+        src_2 = tile_at(ROUNDED_AT[1] + 1024, "src_2", [P, CHUNK], U32)
+        look_up(src_2, x_word_table, src_list, 2, 1)
+        round_groups(nc.scalar.copy, 2, w2_low, 0, 0, W2_HALF)
+        round_groups(nc.scalar.copy, 2, w2_high, W2_HALF, 0, W2_SCALAR)
+        round_groups(nc.vector.tensor_copy, 2, w2_high, W2_HALF, W2_SCALAR, P - W2_HALF)
+
+        y_bank = [psum.tile([P, PACK, CHUNK], F32, name="y%d" % c, tag="y_then_e%d" % c) for c in range(CHUNKS)]
+
+        def passes(bank, codes, scale, row, moving_codes, moving_scale, starts, stops):
             for t in range(PACK):
                 nc.tensor.matmul_mx(
                     out=bank[:, t, :],
                     lhsT=codes[:, cols(t)].bitcast(FP8X4),
                     lhsT_scale=scale[row:P, cols(t)],
-                    rhs=x_codes.bitcast(FP8X4),
-                    rhs_scale=x_scale,
-                    start=opens(t),
-                    stop=closes(t),
+                    rhs=moving_codes.bitcast(FP8X4),
+                    rhs_scale=moving_scale,
+                    start=t in starts,
+                    stop=t in stops,
                 )
 
-        for t in range(PACK):
-            nc.vector.quantize_mx(
-                out=w_codes[2][:, cols(t)].bitcast(FP8X4),
-                scales=w_scale[2][:, cols(t)],
-                in_=grouped[2][:, t, :, :].rearrange("p m j -> p (m j)"),
-            )
-        xs_codes.append(reuse.tile([P, HALF], U32, name="xs_codes1", align_bytes=64, offset=0))
-        xd_codes.append(reuse.tile([P, HALF], U32, name="xd_codes1", align_bytes=64, offset=1024))
-        nc.vector.tensor_copy(xs_codes[1][:], x_table[:].indirect(src_list[:, 16:32]))
-        nc.vector.tensor_copy(xd_codes[1][:], x_table[:].indirect(dst_list[:, 16:32]))
+        for half in range(2):
+            for t in range(PACK):
+                places = slice(t * P + half * W2_HALF, t * P + (half + 1) * W2_HALF)
+                nc.vector.quantize_mx(
+                    out=w_codes[2][:, places].bitcast(FP8X4),
+                    scales=w_scale[2][:, places],
+                    in_=rounded[2][:, t, half * W2_HALF : (half + 1) * W2_HALF, :].rearrange("p m j -> p (m j)"),
+                )
+        src_3 = tile_at(ROUNDED_AT[2], "src_3", [P, CHUNK], U32)
+        look_up(src_3, x_word_table, src_list, 3, 1)
+        dst_23 = tile_at(ROUNDED_AT[2] + 1024, "dst_23", [P, 2 * CHUNK], U32)
+        look_up(dst_23, x_word_table, dst_list, 2, 2)
+        src_codes = [src_01[:, cols(0)], src_01[:, cols(1)], src_2[:], src_3[:]]
+        dst_codes = [dst_01[:, cols(0)], dst_01[:, cols(1)], dst_23[:, cols(0)], dst_23[:, cols(1)]]
+
         for c in range(CHUNKS):
-            passes(acc[c], w_codes[1], w_scale[1], 0, xs_codes[c // 2][:, cols(c % 2)], xs_scale[:, cols(c)], lambda t: t == 0, lambda t: False)
-            passes(acc[c], w_codes[2], w_scale[2], 0, xd_codes[c // 2][:, cols(c % 2)], xd_scale[:, cols(c)], lambda t: False, lambda t: t == PACK - 1)
+            passes(y_bank[c], w_codes[1], w_scale[1], 0, src_codes[c], src_scale[:, cols(c)], {0}, set())
+            passes(y_bank[c], w_codes[2], w_scale[2], 0, dst_codes[c], dst_scale[:, cols(c)], set(), {PACK - 1})
 
         w3_codes = tile("w3_codes", [P, WIDTH], U32)
         w4_codes = tile("w4_codes", [P, WIDTH], U32)
-        w34_scale = reuse.tile([P, WIDTH], U8, name="w34_scale", align_bytes=64, offset=2048)
+        w34_scale = tile_at(ROUNDED_AT[2] + 2048, "w34_scale", [P, WIDTH], U8)
         for dealt, packed in ((w3_codes, w3_raw), (w4_codes, w4_raw)):
             nc.scalar.copy(
                 out=dealt[:].rearrange("p (t m) -> p m t", t=PACK), in_=packed[:].rearrange("p (m t) -> p m t", t=PACK)
             )
         nc.vector.tensor_copy(
-            out=w34_scale[:].rearrange("p (t m) -> p t m", t=PACK), in_=w34_plane[:].rearrange("p (m t) -> p t m", t=PACK)
+            out=w34_scale[:].rearrange("p (t m) -> p t m", t=PACK), in_=w34_scale_raw[:].rearrange("p (m t) -> p t m", t=PACK)
         )
 
-        msg = [ps.tile([P, PACK, CHUNK], F32, name="v%d" % c, tag="msg%d" % c) for c in range(CHUNKS)]
-
+        v_bank = [psum.tile([P, PACK, CHUNK], F32, name="v%d" % c, tag="v%d" % c) for c in range(CHUNKS)]
         out_codes = tile("out_codes", [P, EDGES], U32)
         out_scale = tile("out_scale", [P, EDGES], U8)
-        hidden, score, result, rounded = {}, {}, {}, {}
+        hidden, score, result, result_bf16 = {}, {}, {}, {}
         out_rows = out_0.rearrange("(p t) j -> p t j", t=PACK)
         out_words = as_words(out_1)
+        lone = set(range(PACK))
 
         def leaky(c):
-            y = acc[c][:].rearrange("p t n -> p n t")
-            fifth = tile("fifth%d" % c, [P, CHUNK, PACK], F32)
-            nc.scalar.activation(out=fifth[:], in_=y, func=ACT.Copy, scale=0.2)
+            y = y_bank[c][:].rearrange("p t n -> p n t")
+            sloped = tile("sloped%d" % c, [P, CHUNK, PACK], F32)
+            nc.scalar.activation(out=sloped[:], in_=y, func=ACT.Copy, scale=SLOPE)
             hidden[c] = tile("hidden%d" % c, [P, CHUNK, PACK], BF16)
-            nc.vector.tensor_tensor(out=hidden[c][:], in0=y, in1=fifth[:], op=ALU.max)
+            nc.vector.tensor_tensor(out=hidden[c][:], in0=y, in1=sloped[:], op=ALU.max)
 
-        def scores(c):
+        def products(c):
             h_codes = tile("h_codes%d" % c, [P, CHUNK], U32)
             h_scale = tile("h_scale%d" % c, [P, CHUNK], U8)
             nc.vector.quantize_mx(out=h_codes[:].bitcast(FP8X4), scales=h_scale[:], in_=hidden[c][:].rearrange("p n t -> p (n t)"))
-            bank = ps.tile([P, PACK, CHUNK], F32, name="e%d" % c, tag="acc%d" % c)
-            passes(bank, w3_codes, w34_scale, 0, h_codes[:], h_scale[:], lambda t: True, lambda t: True)
-            passes(msg[c], w4_codes, w34_scale, W4_ROW, xs_codes[c // 2][:, cols(c % 2)], xs_scale[:, cols(c)], lambda t: True, lambda t: True)
+            e_bank = psum.tile([P, PACK, CHUNK], F32, name="e%d" % c, tag="y_then_e%d" % c)
+            passes(e_bank, w3_codes, w34_scale, W3_ROW, h_codes[:], h_scale[:], lone, lone)
+            passes(v_bank[c], w4_codes, w34_scale, W4_ROW, src_codes[c], src_scale[:, cols(c)], lone, lone)
             score[c] = tile("score%d" % c, [P, PACK, CHUNK], F32)
-            nc.scalar.activation(out=score[c][:], in_=bank[:], func=ACT.Tanh)
+            nc.scalar.activation(out=score[c][:], in_=e_bank[:], func=ACT.Tanh)
 
         def weigh(c):
             result[c] = tile("result%d" % c, [P, PACK, CHUNK], F32)
-            nc.vector.tensor_tensor(out=result[c][:], in0=msg[c][:], in1=score[c][:], op=ALU.mult)
+            nc.vector.tensor_tensor(out=result[c][:], in0=v_bank[c][:], in1=score[c][:], op=ALU.mult)
             nc.sync.dma_start(out=out_rows[:, :, cols(c)], in_=result[c][:])
-            rounded[c] = tile("rounded%d" % c, [P, CHUNK, PACK], BF16)
+
+        def round_result(c):
+            result_bf16[c] = tile("result_bf16_%d" % c, [P, CHUNK, PACK], BF16)
             copy = nc.scalar.copy if c < CHUNKS - 1 else nc.vector.tensor_copy
             copy(
-                out=rounded[c][:].rearrange("p (g i) t -> p g t i", i=4),
+                out=result_bf16[c][:].rearrange("p (g i) t -> p g t i", i=4),
                 in_=result[c][:].rearrange("p t (g i) -> p g t i", i=4),
             )
 
         def hand_on(c):
             nc.vector.quantize_mx(
-                out=out_codes[:, cols(c)].bitcast(FP8X4), scales=out_scale[:, cols(c)], in_=rounded[c][:].rearrange("p n t -> p (n t)")
+                out=out_codes[:, cols(c)].bitcast(FP8X4),
+                scales=out_scale[:, cols(c)],
+                in_=result_bf16[c][:].rearrange("p n t -> p (n t)"),
             )
-            nc.sync.dma_start(out=out_words[:, cols(c)], in_=out_codes[:, cols(c)].bitcast(I32))
+            if c % 2 == 1:
+                pair = slice((c - 1) * CHUNK, (c + 1) * CHUNK)
+                nc.sync.dma_start(out=out_words[:, pair], in_=out_codes[:, pair].bitcast(I32))
 
-        stages = (leaky, scores, weigh, hand_on)
-        for step in range(CHUNKS + len(stages) - 1):
-            for lag, stage in enumerate(stages):
+        for step in range(CHUNKS + 2):
+            for lag, stage in ((1, products), (0, leaky), (2, weigh)):
                 if 0 <= step - lag < CHUNKS:
                     stage(step - lag)
+        for c in range(CHUNKS):
+            round_result(c)
+            hand_on(c)
 
-        for q in range(4):
+        for q in range(QUADRANTS):
             engine = nc.sync if q % 2 == 0 else nc.scalar
             engine.dma_start(
                 out=out_2[0, 4 * q : 4 * q + 4, :].bitcast(I32), in_=out_scale[32 * q : 32 * q + 4, :].bitcast(I32)

from contextlib import ExitStack

import concourse.mybir as mybir

FLOPS = 4 * 2 * 512 * 512 * 512

F32 = mybir.dt.float32
BF16 = mybir.dt.bfloat16
I32 = mybir.dt.int32
U32 = mybir.dt.uint32
U16 = mybir.dt.uint16
U8 = mybir.dt.uint8
FP8X4 = mybir.dt.float8_e4m3fn_x4
ACT = mybir.ActivationFunctionType
ALU = mybir.AluOpType

P = 128
PACK = 4
QUADRANTS = 4
NODES = 1024
EDGES = 512
WIDTH = 512
CHUNK = 128
CHUNKS = EDGES // CHUNK
LIST_ROWS = 16
W3_ROW, W4_ROW = 0, 4
SLOPE = 0.2

W1_HEAD = 32
W2_HALF = 64
W2_SCALAR = 20

ROUNDED_AT = {1: 4096, 2: 0}


def tile_picked_zgatt_tanh_po_kernel(
    tc, x_words, x_scales, w1, w2, w3_words, w3_scales, w4_words, w4_scales, offs, dst, out_0, out_1, out_2
):
    nc = tc.nc
    with ExitStack() as ctx:
        held = ctx.enter_context(tc.tile_pool(name="held", bufs=1))
        shared = ctx.enter_context(tc.tile_pool(name="shared", bufs=1))
        psum = ctx.enter_context(tc.psum_pool(name="psum", bufs=1))

        def tile(name, shape, dtype):
            return held.tile(shape, dtype, name=name, align_bytes=64)

        def tile_at(offset, name, shape, dtype):
            return shared.tile(shape, dtype, name=name, align_bytes=64, offset=offset)

        def as_words(packed):
            return packed[0].rearrange("p n t -> p (n t)").bitcast(I32)

        def cols(i):
            return slice(i * P, (i + 1) * P)

        def load_scale_rows(engine, scale_tile, row, scales):
            for q in range(QUADRANTS):
                engine.dma_start(
                    out=scale_tile[32 * q + row : 32 * q + row + 4, :].bitcast(I32),
                    in_=scales[0, 4 * q : 4 * q + 4, :].bitcast(I32),
                )

        src_list = held.tile([P, EDGES // LIST_ROWS], U16, name="src_list")
        dst_list = held.tile([P, EDGES // LIST_ROWS], U16, name="dst_list")
        x_scale_table = tile("x_scale_table", [P, NODES], U8)
        x_word_table = tile("x_word_table", [P, NODES], U32)
        w34_scale_raw = tile("w34_scale_raw", [P, WIDTH], U8)
        nc.gpsimd.memset(x_scale_table[:].bitcast(I32), 0)
        nc.gpsimd.memset(w34_scale_raw[:].bitcast(I32), 0)
        nc.sync.dma_start(src_list[:], offs)
        nc.sync.dma_start(dst_list[:], dst)

        def load_groups(name, w, m0, m1):
            piece = tile(name, [P, PACK, PACK * (m1 - m0)], F32)
            nc.sync.dma_start(out=piece[:], in_=w.rearrange("(p j) c -> p j c", j=PACK)[:, :, PACK * m0 : PACK * m1])
            return piece

        w1_head = load_groups("w1_head", w1, 0, W1_HEAD)
        load_scale_rows(nc.sync, x_scale_table, 0, x_scales)
        w1_rest = load_groups("w1_rest", w1, W1_HEAD, P)
        nc.sync.dma_start(out=x_word_table[:].bitcast(I32), in_=as_words(x_words))
        w2_low = load_groups("w2_low", w2, 0, W2_HALF)
        w2_high = load_groups("w2_high", w2, W2_HALF, P)
        load_scale_rows(nc.gpsimd, w34_scale_raw, W4_ROW, w4_scales)
        w3_raw = tile("w3_raw", [P, WIDTH], U32)
        w4_raw = tile("w4_raw", [P, WIDTH], U32)
        nc.sync.dma_start(out=w3_raw[:].bitcast(I32), in_=as_words(w3_words))
        load_scale_rows(nc.sync, w34_scale_raw, W3_ROW, w3_scales)
        nc.sync.dma_start(out=w4_raw[:].bitcast(I32), in_=as_words(w4_words))

        def look_up(gathered, table, entries, first_chunk, chunks):
            per_chunk = CHUNK // LIST_ROWS
            offsets = entries[:, first_chunk * per_chunk : (first_chunk + chunks) * per_chunk]
            nc.vector.tensor_copy(gathered[:], table[:].indirect(offsets))

        src_scale = tile("src_scale", [P, EDGES], U8)
        dst_scale = tile("dst_scale", [P, EDGES], U8)
        src_01 = tile("src_01", [P, 2 * CHUNK], U32)
        look_up(src_scale, x_scale_table, src_list, 0, CHUNKS)
        look_up(dst_scale, x_scale_table, dst_list, 0, CHUNKS)
        look_up(src_01, x_word_table, src_list, 0, 2)

        rounded = {w: tile_at(ROUNDED_AT[w], "rounded%d" % w, [P, PACK, P, PACK], BF16) for w in (1, 2)}
        w_codes = {w: tile("w_codes%d" % w, [P, WIDTH], U32) for w in (1, 2)}
        w_scale = {w: tile("w_scale%d" % w, [P, WIDTH], U8) for w in (1, 2)}

        def round_groups(copy, w, piece, first, m0, m1):
            copy(
                out=rounded[w][:, :, first + m0 : first + m1, :].rearrange("p t m j -> p m j t"),
                in_=piece[:, :, PACK * m0 : PACK * m1].rearrange("p j (m t) -> p m j t", t=PACK),
            )

        round_groups(nc.scalar.copy, 1, w1_head, 0, 0, W1_HEAD)
        round_groups(nc.scalar.copy, 1, w1_rest, W1_HEAD, 0, P - W1_HEAD)
        nc.vector.quantize_mx(
            out=w_codes[1][:].bitcast(FP8X4), scales=w_scale[1][:], in_=rounded[1][:].rearrange("p t m j -> p (t m j)")
        )
        dst_01 = tile_at(ROUNDED_AT[1], "dst_01", [P, 2 * CHUNK], U32)
        look_up(dst_01, x_word_table, dst_list, 0, 2)
        src_2 = tile_at(ROUNDED_AT[1] + 1024, "src_2", [P, CHUNK], U32)
        look_up(src_2, x_word_table, src_list, 2, 1)
        round_groups(nc.scalar.copy, 2, w2_low, 0, 0, W2_HALF)
        round_groups(nc.scalar.copy, 2, w2_high, W2_HALF, 0, W2_SCALAR)
        round_groups(nc.vector.tensor_copy, 2, w2_high, W2_HALF, W2_SCALAR, P - W2_HALF)

        y_bank = [psum.tile([P, PACK, CHUNK], F32, name="y%d" % c, tag="y_then_e%d" % c) for c in range(CHUNKS)]

        def passes(bank, codes, scale, row, moving_codes, moving_scale, starts, stops):
            for t in range(PACK):
                nc.tensor.matmul_mx(
                    out=bank[:, t, :],
                    lhsT=codes[:, cols(t)].bitcast(FP8X4),
                    lhsT_scale=scale[row:P, cols(t)],
                    rhs=moving_codes.bitcast(FP8X4),
                    rhs_scale=moving_scale,
                    start=t in starts,
                    stop=t in stops,
                )

        for half in range(2):
            for t in range(PACK):
                places = slice(t * P + half * W2_HALF, t * P + (half + 1) * W2_HALF)
                nc.vector.quantize_mx(
                    out=w_codes[2][:, places].bitcast(FP8X4),
                    scales=w_scale[2][:, places],
                    in_=rounded[2][:, t, half * W2_HALF : (half + 1) * W2_HALF, :].rearrange("p m j -> p (m j)"),
                )
        src_3 = tile_at(ROUNDED_AT[2], "src_3", [P, CHUNK], U32)
        look_up(src_3, x_word_table, src_list, 3, 1)
        dst_23 = tile_at(ROUNDED_AT[2] + 1024, "dst_23", [P, 2 * CHUNK], U32)
        look_up(dst_23, x_word_table, dst_list, 2, 2)
        src_codes = [src_01[:, cols(0)], src_01[:, cols(1)], src_2[:], src_3[:]]
        dst_codes = [dst_01[:, cols(0)], dst_01[:, cols(1)], dst_23[:, cols(0)], dst_23[:, cols(1)]]

        for c in range(CHUNKS):
            passes(y_bank[c], w_codes[1], w_scale[1], 0, src_codes[c], src_scale[:, cols(c)], {0}, set())
            passes(y_bank[c], w_codes[2], w_scale[2], 0, dst_codes[c], dst_scale[:, cols(c)], set(), {PACK - 1})

        w3_codes = tile("w3_codes", [P, WIDTH], U32)
        w4_codes = tile("w4_codes", [P, WIDTH], U32)
        w34_scale = tile_at(ROUNDED_AT[2] + 2048, "w34_scale", [P, WIDTH], U8)
        for dealt, packed in ((w3_codes, w3_raw), (w4_codes, w4_raw)):
            nc.scalar.copy(
                out=dealt[:].rearrange("p (t m) -> p m t", t=PACK), in_=packed[:].rearrange("p (m t) -> p m t", t=PACK)
            )
        nc.vector.tensor_copy(
            out=w34_scale[:].rearrange("p (t m) -> p t m", t=PACK), in_=w34_scale_raw[:].rearrange("p (m t) -> p t m", t=PACK)
        )

        v_bank = [psum.tile([P, PACK, CHUNK], F32, name="v%d" % c, tag="v%d" % c) for c in range(CHUNKS)]
        out_codes = tile("out_codes", [P, EDGES], U32)
        out_scale = tile("out_scale", [P, EDGES], U8)
        hidden, score, result, result_bf16 = {}, {}, {}, {}
        out_rows = out_0.rearrange("(p t) j -> p t j", t=PACK)
        out_words = as_words(out_1)
        lone = set(range(PACK))

        def leaky(c):
            y = y_bank[c][:].rearrange("p t n -> p n t")
            sloped = tile("sloped%d" % c, [P, CHUNK, PACK], F32)
            nc.scalar.activation(out=sloped[:], in_=y, func=ACT.Copy, scale=SLOPE)
            hidden[c] = tile("hidden%d" % c, [P, CHUNK, PACK], BF16)
            nc.vector.tensor_tensor(out=hidden[c][:], in0=y, in1=sloped[:], op=ALU.max)

        def products(c):
            h_codes = tile("h_codes%d" % c, [P, CHUNK], U32)
            h_scale = tile("h_scale%d" % c, [P, CHUNK], U8)
            nc.vector.quantize_mx(out=h_codes[:].bitcast(FP8X4), scales=h_scale[:], in_=hidden[c][:].rearrange("p n t -> p (n t)"))
            e_bank = psum.tile([P, PACK, CHUNK], F32, name="e%d" % c, tag="y_then_e%d" % c)
            passes(e_bank, w3_codes, w34_scale, W3_ROW, h_codes[:], h_scale[:], lone, lone)
            passes(v_bank[c], w4_codes, w34_scale, W4_ROW, src_codes[c], src_scale[:, cols(c)], lone, lone)
            score[c] = tile("score%d" % c, [P, PACK, CHUNK], F32)
            nc.scalar.activation(out=score[c][:], in_=e_bank[:], func=ACT.Tanh)

        def weigh(c):
            result[c] = tile("result%d" % c, [P, PACK, CHUNK], F32)
            nc.vector.tensor_tensor(out=result[c][:], in0=v_bank[c][:], in1=score[c][:], op=ALU.mult)
            nc.sync.dma_start(out=out_rows[:, :, cols(c)], in_=result[c][:])

        def round_result(c):
            result_bf16[c] = tile("result_bf16_%d" % c, [P, CHUNK, PACK], BF16)
            copy = nc.scalar.copy if c < CHUNKS - 1 else nc.vector.tensor_copy
            copy(
                out=result_bf16[c][:].rearrange("p (g i) t -> p g t i", i=4),
                in_=result[c][:].rearrange("p t (g i) -> p g t i", i=4),
            )

        def hand_on(c):
            nc.vector.quantize_mx(
                out=out_codes[:, cols(c)].bitcast(FP8X4),
                scales=out_scale[:, cols(c)],
                in_=result_bf16[c][:].rearrange("p n t -> p (n t)"),
            )
            if c % 2 == 1:
                pair = slice((c - 1) * CHUNK, (c + 1) * CHUNK)
                nc.sync.dma_start(out=out_words[:, pair], in_=out_codes[:, pair].bitcast(I32))

        for step in range(CHUNKS + 2):
            for lag, stage in ((1, products), (0, leaky), (2, weigh)):
                if 0 <= step - lag < CHUNKS:
                    stage(step - lag)
        for c in range(CHUNKS):
            round_result(c)
            hand_on(c)

        for q in range(QUADRANTS):
            engine = nc.sync if q % 2 == 0 else nc.scalar
            engine.dma_start(
                out=out_2[0, 4 * q : 4 * q + 4, :].bitcast(I32), in_=out_scale[32 * q : 32 * q + 4, :].bitcast(I32)
            )
